import numpy as np
import ml_dtypes


def mxq(x, axis, fmt="e4m3"):
    dtype, down = {"e4m3": (ml_dtypes.float8_e4m3fn, 7), "e5m2": (ml_dtypes.float8_e5m2, 14)}[fmt]
    v = np.moveaxis(np.asarray(x, np.float32).astype(ml_dtypes.bfloat16).astype(np.float64), axis, -1)
    blocks = v.reshape(v.shape[:-1] + (-1, 32))
    amax = np.abs(blocks).max(-1, keepdims=True)
    byte = np.maximum(np.where(amax > 0, np.frexp(amax)[1] - 1 + 127, 0) - down, 1)
    scale = np.exp2(byte - 127.0)
    codes = (blocks / scale).astype(np.float32).astype(dtype).astype(np.float64)
    return np.moveaxis((codes * scale).reshape(v.shape), -1, axis)


WIDE = False


def mx_kscale(k):
    if not WIDE:
        return np.ones(k)
    levels = np.array([30, -30])
    if k % 512:
        return np.exp2(np.random.permutation(np.resize(levels, k // 32))).repeat(32)
    a = np.empty((k // 512, 16))
    for p in range(k // 512):
        a[p, :8] = np.random.permutation(np.resize(levels, 8))
        for g in range(8):
            far = levels[np.abs(levels - a[p, g]) >= 10]
            a[p, g + 8] = far[np.random.randint(len(far))]
    return np.exp2(a.ravel()).repeat(32)


def f64(x):
    return np.asarray(x).astype(np.float64)


def striped(idx):
    return np.tile(np.asarray(idx).reshape(-1, 16).T, (8, 1)).astype(np.uint16)


def unstriped(offs):
    return offs[:16].T.reshape(-1).astype(np.int64)


E2M1 = np.array([0.0, 0.5, 1.0, 1.5, 2.0, 3.0, 4.0, 6.0, -0.0, -0.5, -1.0, -1.5, -2.0, -3.0, -4.0, -6.0])


def pack_weight(w, fmt):
    k, n = w.shape
    w = f64(np.asarray(w, np.float32).astype(ml_dtypes.bfloat16)).reshape(k // 32, 32, n)
    amax = np.abs(w).max(1)
    if fmt in ("e4m3", "e5m2"):
        byte = np.frexp(amax)[1] - 1 + 127 - (7 if fmt == "e4m3" else 14)
    else:
        mant, ex = np.frexp(amax / 6.0)
        byte = np.where(mant > 0.5, ex, ex - 1) + 127
    byte = np.clip(np.where(amax > 0, byte, 1), 1, 254)
    scaled = (w * np.exp2(127.0 - byte)[:, None, :]).reshape(k, n).astype(np.float32)
    by_word = np.ascontiguousarray(scaled.reshape(k // 512, 128, 4, n).transpose(0, 1, 3, 2))
    if fmt in ("e4m3", "e5m2"):
        words = by_word.astype(ml_dtypes.float8_e4m3fn if fmt == "e4m3" else ml_dtypes.float8_e5m2).view(np.uint8)
    else:
        c = by_word.astype(ml_dtypes.float4_e2m1fn).view(np.uint8) & 0xF
        words = (c[..., 0::2] | (c[..., 1::2] << 4)).reshape(k // 512, 128, 2 * n)
    return np.ascontiguousarray(words), np.ascontiguousarray(byte.astype(np.uint8).reshape(k // 512, 16, n))


def unpack_weight(words, scales, fmt):
    g, _, n = scales.shape
    words = np.ascontiguousarray(words).reshape(g, 128, n, -1)
    if fmt in ("e4m3", "e5m2"):
        vals = words.view(ml_dtypes.float8_e4m3fn if fmt == "e4m3" else ml_dtypes.float8_e5m2).astype(np.float64)
    else:
        nib = np.empty((g, 128, n, 4), np.uint8)
        nib[..., 0::2] = words & 0xF
        nib[..., 1::2] = words >> 4
        vals = E2M1[nib]
    vals = vals * np.repeat(np.exp2(scales.astype(np.float64) - 127.0), 8, axis=1)[..., None]
    return vals.transpose(0, 1, 3, 2).reshape(g * 512, n)


def bf(x):
    return np.asarray(x, np.float32).astype(ml_dtypes.bfloat16)


def planes(Y):
    r, m = Y.shape
    b = f64(bf(Y)).reshape(r // 32, 32, m)
    amax = np.abs(b).max(1)
    byte = np.clip(np.where(amax > 0, np.frexp(amax)[1] - 1 + 127 - 7, 1), 1, 254)
    codes = (b * np.exp2(127.0 - byte)[:, None, :]).reshape(r, m).astype(np.float32).astype(ml_dtypes.float8_e4m3fn).view(np.uint8)
    words = codes.reshape(r // 512, 128, 4, m).transpose(0, 1, 3, 2)
    return np.ascontiguousarray(words), np.ascontiguousarray(byte.astype(np.uint8).reshape(r // 512, 16, m))


K, J, N, T, B = 512, 512, 256, 1024, 64


def setup_inputs():
    n = np.random.standard_normal
    idx = np.random.permutation(T)[:J]
    fj = mx_kscale(J)
    gjp = pack_weight(n((J, N)) * np.exp(0.5 * n((J, 1))) / fj[:, None], "e5m2")
    return {
        "xf": (n((K, T))).astype(np.float32),
        "ra": (np.random.uniform(0.5, 1.5, (1, J)) * fj).astype(np.float32),
        "gj_words": gjp[0],
        "gj_scales": gjp[1],
        "old": (12.0 * n((K, N))).astype(np.float32),
        "offs": striped(idx),
    }


def reference(xf, ra, gj_words, gj_scales, old, offs):
    idx = unstriped(offs)
    gju = unpack_weight(gj_words, gj_scales, "e5m2")
    xg = f64(xf)[:, idx]
    g1 = xg.reshape(K, B, J // B).mean(axis=2)
    g2 = np.repeat(g1, J // B, axis=1)
    us = (xg - g2) * f64(ra)
    uj = us.T
    ujq = mxq(uj, 0, "e5m2")
    w = ujq.T @ gju
    y = 0.04 * np.maximum(w, f64(old))
    words, scales = planes(y)
    return y, words, scales

@@ -1,0 +1,120 @@
+from contextlib import ExitStack
+
+import concourse.mybir as mybir
+from concourse.masks import make_identity
+
+K, J, N, T = 512, 512, 256, 1024
+FLOPS = 2 * K * J * N
+
+F32 = mybir.dt.float32
+BF16 = mybir.dt.bfloat16
+I32 = mybir.dt.int32
+U32 = mybir.dt.uint32
+U16 = mybir.dt.uint16
+U8 = mybir.dt.uint8
+E5M2X4 = mybir.dt.float8_e5m2_x4
+E4M3X4 = mybir.dt.float8_e4m3fn_x4
+ALU = mybir.AluOpType
+COPY = mybir.ActivationFunctionType.Copy
+
+P = 128
+PACK = 4
+GROUP = 8
+GROUPS = J // GROUP
+KEEP = 0.04
+
+
+def tile_list_moment_centred_stored_larger_pl_kernel(tc, xf, ra, gj_words, gj_scales, old, offs, out_0, out_1, out_2):
+    nc = tc.nc
+    with ExitStack() as ctx:
+        held = ctx.enter_context(tc.tile_pool(name="held", bufs=1))
+        psum = ctx.enter_context(tc.psum_pool(name="psum", bufs=1))
+
+        offsets = held.tile([P, J // 16], U16, name="offsets")
+
+        xf_dealt = xf.rearrange("(p t) c -> p t c", t=PACK)
+        table = [held.tile([P, T], F32, name="table%d" % t) for t in range(PACK)]
+        weight = held.tile([P, PACK], F32, name="weight")
+        g_words = held.tile([P, N], U32, name="g_words", align_bytes=64)
+        g_scales = held.tile([P, N], U8, name="g_scales", align_bytes=64)
+        old_rows = held.tile([P, PACK, N], F32, name="old_rows")
+
+        nc.vector.memset(g_scales[:].bitcast(U32), 0)
+        nc.sync.dma_start(table[0][:], xf_dealt[:, 0, :])
+        nc.sync.dma_start(offsets[:], offs)
+        for q in range(4):
+            nc.sync.dma_start(g_scales[32 * q : 32 * q + 4, :].bitcast(I32), gj_scales[0, 4 * q : 4 * q + 4, :].bitcast(I32))
+        nc.sync.dma_start(table[1][:], xf_dealt[:, 1, :])
+        nc.sync.dma_start(weight[:], ra.rearrange("o (p r) -> (o p) r", r=PACK))
+        nc.sync.dma_start(table[2][:], xf_dealt[:, 2, :])
+        nc.sync.dma_start(g_words[:].bitcast(I32), gj_words[0].rearrange("p n r -> p (n r)").bitcast(I32))
+        nc.sync.dma_start(table[3][:], xf_dealt[:, 3, :])
+        nc.sync.dma_start(old_rows[:], old.rearrange("(p t) n -> p t n", t=PACK))
+
+        identity = held.tile([P, P], F32, name="identity")
+        make_identity(nc, identity[:])
+
+        y = held.tile([P, PACK, N], F32, name="y")
+        y_bf = held.tile([P, N, PACK], BF16, name="y_bf", align_bytes=64)
+        old_kept = held.tile([P, PACK, N], F32, name="old_kept")
+        out_dealt = out_0.rearrange("(p t) n -> p t n", t=PACK)
+
+        for t in range(PACK):
+            picked = held.tile([P, J], F32, name="picked%d" % t)
+            if t == 0:
+                half = J // 2
+                nc.scalar.activation(picked[:, :half], table[t][:].indirect(offsets[:, : half // 16]), COPY)
+                nc.vector.tensor_copy(picked[:, half:], table[t][:].indirect(offsets[:, half // 16 :]))
+            else:
+                nc.scalar.activation(picked[:], table[t][:].indirect(offsets[:]), COPY)
+
+            sums = held.tile([P, GROUPS], F32, name="sums%d" % t)
+            nc.vector.tensor_reduce(sums[:], picked[:].rearrange("p (b i) -> p b i", i=GROUP), mybir.AxisListType.X, ALU.add)
+
+            centred = held.tile([P, 2, P, 2], F32, name="centred%d" % t)
+            by_pair = picked[:].rearrange("p (q u e) -> p u q e", u=2, e=2)
+            spread = sums[:].unsqueeze(2).to_broadcast([P, GROUPS, 4])
+            for u in range(2):
+                nc.vector.scalar_tensor_tensor(
+                    centred[:, u], spread, -1.0 / GROUP, by_pair[:, u], ALU.mult, ALU.add
+                )
+
+            turned = psum.tile([P, PACK, P], F32, name="turned%d" % t)
+            for r in range(PACK):
+                nc.tensor.transpose(turned[:, r, :], centred[:, r // 2, :, r % 2], identity[:])
+
+            u_bf = held.tile([P, P, PACK], BF16, name="u_bf%d" % t, align_bytes=64)
+            nc.vector.tensor_tensor(
+                u_bf[:], turned[:].rearrange("p r k -> p k r"), weight[:].unsqueeze(1).to_broadcast([P, P, PACK]), ALU.mult
+            )
+            u_words = held.tile([P, P], U32, name="u_words%d" % t, align_bytes=64)
+            u_scales = held.tile([P, P], U8, name="u_scales%d" % t, align_bytes=64)
+            nc.vector.quantize_mx(u_words[:].bitcast(E5M2X4), u_scales[:], u_bf[:].rearrange("p k r -> p (k r)"))
+
+            moment = psum.tile([P, N], F32, name="moment%d" % t)
+            nc.tensor.matmul_mx(
+                moment[:],
+                lhsT=u_words[:].bitcast(E5M2X4),
+                lhsT_scale=u_scales[:],
+                rhs=g_words[:].bitcast(E5M2X4),
+                rhs_scale=g_scales[:],
+                start=True,
+                stop=True,
+            )
+
+            nc.scalar.activation(old_kept[:, t, :], old_rows[:, t, :], COPY, scale=KEEP)
+            nc.vector.scalar_tensor_tensor(y[:, t, :], moment[:], KEEP, old_kept[:, t, :], ALU.mult, ALU.max)
+            if t == 1:
+                nc.sync.dma_start(out_dealt[:, 0:2, :], y[:, 0:2, :])
+                nc.scalar.copy(y_bf[:, :, 0:2], y[:, 0:2, :].rearrange("p t n -> p n t"))
+            if t >= 2:
+                nc.sync.dma_start(out_dealt[:, t, :], y[:, t, :])
+
+        nc.vector.tensor_copy(y_bf[:, :, 2:4], y[:, 2:4, :].rearrange("p t n -> p n t"))
+        y_words = held.tile([P, N], U32, name="y_words", align_bytes=64)
+        y_scales = held.tile([P, N], U8, name="y_scales", align_bytes=64)
+        nc.vector.quantize_mx(y_words[:].bitcast(E4M3X4), y_scales[:], y_bf[:].rearrange("p n t -> p (n t)"))
+        nc.sync.dma_start(out_1[0].rearrange("p n r -> p (n r)").bitcast(I32), y_words[:].bitcast(I32))
+        for q in range(4):
+            queue = nc.scalar if q % 2 == 0 else nc.sync
+            queue.dma_start(out_2[0, 4 * q : 4 * q + 4, :].bitcast(I32), y_scales[32 * q : 32 * q + 4, :].bitcast(I32))

@@ -42,73 +42,119 @@ def tile_list_moment_centred_stored_larger_pl_kernel(tc, xf, ra, gj_words, gj_sc
         nc.vector.memset(g_scales[:].bitcast(U32), 0)
         nc.sync.dma_start(table[0][:], xf_dealt[:, 0, :])
         nc.sync.dma_start(offsets[:], offs)
+        for t in range(1, PACK):
+            nc.sync.dma_start(table[t][:], xf_dealt[:, t, :])
+        nc.sync.dma_start(weight[:], ra.rearrange("o (p r) -> (o p) r", r=PACK))
+        nc.sync.dma_start(g_words[:].bitcast(I32), gj_words[0].rearrange("p n r -> p (n r)").bitcast(I32))
+        nc.sync.dma_start(old_rows[:], old.rearrange("(p t) n -> p t n", t=PACK))
         for q in range(4):
             nc.sync.dma_start(g_scales[32 * q : 32 * q + 4, :].bitcast(I32), gj_scales[0, 4 * q : 4 * q + 4, :].bitcast(I32))
-        nc.sync.dma_start(table[1][:], xf_dealt[:, 1, :])
-        nc.sync.dma_start(weight[:], ra.rearrange("o (p r) -> (o p) r", r=PACK))
-        nc.sync.dma_start(table[2][:], xf_dealt[:, 2, :])
-        nc.sync.dma_start(g_words[:].bitcast(I32), gj_words[0].rearrange("p n r -> p (n r)").bitcast(I32))
-        nc.sync.dma_start(table[3][:], xf_dealt[:, 3, :])
-        nc.sync.dma_start(old_rows[:], old.rearrange("(p t) n -> p t n", t=PACK))
 
         identity = held.tile([P, P], F32, name="identity")
-        make_identity(nc, identity[:])
+        nc.any.memset(identity[:], 0.0)
+        make_identity(nc, identity[:], nomemset=True)
 
         y = held.tile([P, PACK, N], F32, name="y")
         y_bf = held.tile([P, N, PACK], BF16, name="y_bf", align_bytes=64)
         old_kept = held.tile([P, PACK, N], F32, name="old_kept")
         out_dealt = out_0.rearrange("(p t) n -> p t n", t=PACK)
 
-        for t in range(PACK):
-            picked = held.tile([P, J], F32, name="picked%d" % t)
+        picked = [held.tile([P, J], F32, name="picked%d" % t) for t in range(PACK)]
+        sums = [held.tile([P, GROUPS], F32, name="sums%d" % t) for t in range(PACK)]
+        turned = [psum.tile([P, PACK, P], F32, name="turned%d" % t) for t in range(PACK)]
+        u_bf = held.tile([P, PACK, P * PACK], BF16, name="u_bf", align_bytes=64)
+        u_words = held.tile([P, PACK * P], U32, name="u_words", align_bytes=64)
+        u_scales = held.tile([P, PACK * P], U8, name="u_scales", align_bytes=64)
+        moment_01 = psum.tile([P, 2, N], F32, name="moment_01")
+        moment_2 = psum.tile([P, N], F32, name="moment_2")
+        moment_3 = psum.tile([P, N], F32, name="moment_3")
+        moment = [moment_01[:, 0, :], moment_01[:, 1, :], moment_2[:], moment_3[:]]
+
+        def gather(t):
             if t == 0:
                 half = J // 2
-                nc.scalar.activation(picked[:, :half], table[t][:].indirect(offsets[:, : half // 16]), COPY)
-                nc.vector.tensor_copy(picked[:, half:], table[t][:].indirect(offsets[:, half // 16 :]))
+                nc.scalar.activation(picked[t][:, :half], table[t][:].indirect(offsets[:, : half // 16]), COPY)
+                nc.vector.tensor_copy(picked[t][:, half:], table[t][:].indirect(offsets[:, half // 16 :]))
             else:
-                nc.scalar.activation(picked[:], table[t][:].indirect(offsets[:]), COPY)
+                nc.scalar.activation(picked[t][:], table[t][:].indirect(offsets[:]), COPY)
 
-            sums = held.tile([P, GROUPS], F32, name="sums%d" % t)
-            nc.vector.tensor_reduce(sums[:], picked[:].rearrange("p (b i) -> p b i", i=GROUP), mybir.AxisListType.X, ALU.add)
+        def group_sums(t):
+            nc.vector.tensor_reduce(sums[t][:], picked[t][:].rearrange("p (b i) -> p b i", i=GROUP), mybir.AxisListType.X, ALU.add)
 
+        def centre_and_turn(t):
             centred = held.tile([P, 2, P, 2], F32, name="centred%d" % t)
-            by_pair = picked[:].rearrange("p (q u e) -> p u q e", u=2, e=2)
-            spread = sums[:].unsqueeze(2).to_broadcast([P, GROUPS, 4])
+            by_pair = picked[t][:].rearrange("p (q u e) -> p u q e", u=2, e=2)
+            spread = sums[t][:].unsqueeze(2).to_broadcast([P, GROUPS, 4])
             for u in range(2):
-                nc.vector.scalar_tensor_tensor(
-                    centred[:, u], spread, -1.0 / GROUP, by_pair[:, u], ALU.mult, ALU.add
+                nc.vector.scalar_tensor_tensor(centred[:, u], spread, -1.0 / GROUP, by_pair[:, u], ALU.mult, ALU.add)
+            for r in range(PACK):
+                nc.tensor.transpose(turned[t][:, r, :], centred[:, r // 2, :, r % 2], identity[:])
+
+        def turn_picked(t):
+            by_slot = picked[t][:].rearrange("p (q r) -> p r q", r=PACK)
+            for r in range(PACK):
+                nc.tensor.matmul(turned[t][:, r, :], by_slot[:, r, :], identity[:], start=(r == 0), stop=False, is_transpose=True)
+
+        def add_turned_means(t):
+            less_mean = held.tile([P, GROUPS, 2], F32, name="less_mean%d" % t)
+            nc.vector.tensor_scalar(less_mean[:], sums[t][:].unsqueeze(2).to_broadcast([P, GROUPS, 2]), -1.0 / GROUP, None, ALU.mult)
+            for r in range(PACK):
+                nc.tensor.matmul(
+                    turned[t][:, r, :], less_mean[:].rearrange("p b h -> p (b h)"), identity[:], start=False, stop=(r == PACK - 1), is_transpose=True
                 )
 
-            turned = psum.tile([P, PACK, P], F32, name="turned%d" % t)
-            for r in range(PACK):
-                nc.tensor.transpose(turned[:, r, :], centred[:, r // 2, :, r % 2], identity[:])
-
-            u_bf = held.tile([P, P, PACK], BF16, name="u_bf%d" % t, align_bytes=64)
+        def weigh(t):
             nc.vector.tensor_tensor(
-                u_bf[:], turned[:].rearrange("p r k -> p k r"), weight[:].unsqueeze(1).to_broadcast([P, P, PACK]), ALU.mult
-            )
-            u_words = held.tile([P, P], U32, name="u_words%d" % t, align_bytes=64)
-            u_scales = held.tile([P, P], U8, name="u_scales%d" % t, align_bytes=64)
-            nc.vector.quantize_mx(u_words[:].bitcast(E5M2X4), u_scales[:], u_bf[:].rearrange("p k r -> p (k r)"))
-
-            moment = psum.tile([P, N], F32, name="moment%d" % t)
-            nc.tensor.matmul_mx(
-                moment[:],
-                lhsT=u_words[:].bitcast(E5M2X4),
-                lhsT_scale=u_scales[:],
-                rhs=g_words[:].bitcast(E5M2X4),
-                rhs_scale=g_scales[:],
-                start=True,
-                stop=True,
+                u_bf[:, t, :].rearrange("p (k r) -> p k r", r=PACK),
+                turned[t][:].rearrange("p r k -> p k r"),
+                weight[:].unsqueeze(1).to_broadcast([P, P, PACK]),
+                ALU.mult,
             )
 
+        def multiply(first, last):
+            cols = slice(first * P, last * P)
+            nc.vector.quantize_mx(u_words[:, cols].bitcast(E5M2X4), u_scales[:, cols], u_bf[:, first:last, :].rearrange("p t c -> p (t c)"))
+            for t in range(first, last):
+                cols = slice(t * P, (t + 1) * P)
+                nc.tensor.matmul_mx(
+                    moment[t],
+                    lhsT=u_words[:, cols].bitcast(E5M2X4),
+                    lhsT_scale=u_scales[:, cols],
+                    rhs=g_words[:].bitcast(E5M2X4),
+                    rhs_scale=g_scales[:],
+                    start=True,
+                    stop=True,
+                )
+
+        def keep_larger(sums_in_psum, first, last):
+            nc.vector.scalar_tensor_tensor(y[:, first:last, :], sums_in_psum, KEEP, old_kept[:, first:last, :], ALU.mult, ALU.max)
+            nc.sync.dma_start(out_dealt[:, first:last, :], y[:, first:last, :])
+
+        for t in range(PACK):
+            gather(t)
+        for t in range(PACK):
             nc.scalar.activation(old_kept[:, t, :], old_rows[:, t, :], COPY, scale=KEEP)
-            nc.vector.scalar_tensor_tensor(y[:, t, :], moment[:], KEEP, old_kept[:, t, :], ALU.mult, ALU.max)
-            if t == 1:
-                nc.sync.dma_start(out_dealt[:, 0:2, :], y[:, 0:2, :])
-                nc.scalar.copy(y_bf[:, :, 0:2], y[:, 0:2, :].rearrange("p t n -> p n t"))
-            if t >= 2:
-                nc.sync.dma_start(out_dealt[:, t, :], y[:, t, :])
+        group_sums(0)
+        centre_and_turn(0)
+        group_sums(1)
+        turn_picked(2)
+        centre_and_turn(1)
+        group_sums(2)
+        turn_picked(3)
+        weigh(0)
+        add_turned_means(2)
+        group_sums(3)
+        weigh(1)
+        add_turned_means(3)
+        multiply(0, 2)
+        weigh(2)
+        weigh(3)
+        multiply(2, 3)
+        multiply(3, 4)
+        keep_larger(moment_01[:], 0, 2)
+        nc.scalar.copy(y_bf[:, :, 0:2], y[:, 0:2, :].rearrange("p t n -> p n t"))
+        keep_larger(moment_2[:].unsqueeze(1), 2, 3)
+        keep_larger(moment_3[:].unsqueeze(1), 3, 4)
 
         nc.vector.tensor_copy(y_bf[:, :, 2:4], y[:, 2:4, :].rearrange("p t n -> p n t"))
         y_words = held.tile([P, N], U32, name="y_words", align_bytes=64)

@@ -33,7 +33,7 @@ def tile_list_moment_centred_stored_larger_pl_kernel(tc, xf, ra, gj_words, gj_sc
         offsets = held.tile([P, J // 16], U16, name="offsets")
 
         xf_dealt = xf.rearrange("(p t) c -> p t c", t=PACK)
-        table = [held.tile([P, T], F32, name="table%d" % t) for t in range(PACK)]
+        table = [held.tile([P, T], F32, name="table%d" % t, tag="table%d" % t, align_bytes=64) for t in range(PACK)]
         weight = held.tile([P, PACK], F32, name="weight")
         g_words = held.tile([P, N], U32, name="g_words", align_bytes=64)
         g_scales = held.tile([P, N], U8, name="g_scales", align_bytes=64)
@@ -42,9 +42,9 @@ def tile_list_moment_centred_stored_larger_pl_kernel(tc, xf, ra, gj_words, gj_sc
         nc.vector.memset(g_scales[:].bitcast(U32), 0)
         nc.sync.dma_start(table[0][:], xf_dealt[:, 0, :])
         nc.sync.dma_start(offsets[:], offs)
+        nc.sync.dma_start(weight[:], ra.rearrange("o (p r) -> (o p) r", r=PACK))
         for t in range(1, PACK):
             nc.sync.dma_start(table[t][:], xf_dealt[:, t, :])
-        nc.sync.dma_start(weight[:], ra.rearrange("o (p r) -> (o p) r", r=PACK))
         nc.sync.dma_start(g_words[:].bitcast(I32), gj_words[0].rearrange("p n r -> p (n r)").bitcast(I32))
         nc.sync.dma_start(old_rows[:], old.rearrange("(p t) n -> p t n", t=PACK))
         for q in range(4):
@@ -54,17 +54,12 @@ def tile_list_moment_centred_stored_larger_pl_kernel(tc, xf, ra, gj_words, gj_sc
         nc.any.memset(identity[:], 0.0)
         make_identity(nc, identity[:], nomemset=True)
 
-        y = held.tile([P, PACK, N], F32, name="y")
         y_bf = held.tile([P, N, PACK], BF16, name="y_bf", align_bytes=64)
-        old_kept = held.tile([P, PACK, N], F32, name="old_kept")
         out_dealt = out_0.rearrange("(p t) n -> p t n", t=PACK)
 
         picked = [held.tile([P, J], F32, name="picked%d" % t) for t in range(PACK)]
-        sums = [held.tile([P, GROUPS], F32, name="sums%d" % t) for t in range(PACK)]
+        sums = [held.tile([P, GROUPS], F32, name="sums%d" % t, tag="sums%d" % t, align_bytes=64) for t in range(PACK)]
         turned = [psum.tile([P, PACK, P], F32, name="turned%d" % t) for t in range(PACK)]
-        u_bf = held.tile([P, PACK, P * PACK], BF16, name="u_bf", align_bytes=64)
-        u_words = held.tile([P, PACK * P], U32, name="u_words", align_bytes=64)
-        u_scales = held.tile([P, PACK * P], U8, name="u_scales", align_bytes=64)
         moment_01 = psum.tile([P, 2, N], F32, name="moment_01")
         moment_2 = psum.tile([P, N], F32, name="moment_2")
         moment_3 = psum.tile([P, N], F32, name="moment_3")
@@ -103,21 +98,26 @@ def tile_list_moment_centred_stored_larger_pl_kernel(tc, xf, ra, gj_words, gj_sc
                     turned[t][:, r, :], less_mean[:].rearrange("p b h -> p (b h)"), identity[:], start=False, stop=(r == PACK - 1), is_transpose=True
                 )
 
-        def weigh(t):
+        def weigh(t, dst):
             nc.vector.tensor_tensor(
-                u_bf[:, t, :].rearrange("p (k r) -> p k r", r=PACK),
+                dst.rearrange("p (k r) -> p k r", r=PACK),
                 turned[t][:].rearrange("p r k -> p k r"),
                 weight[:].unsqueeze(1).to_broadcast([P, P, PACK]),
                 ALU.mult,
             )
 
-        def multiply(first, last):
-            cols = slice(first * P, last * P)
-            nc.vector.quantize_mx(u_words[:, cols].bitcast(E5M2X4), u_scales[:, cols], u_bf[:, first:last, :].rearrange("p t c -> p (t c)"))
-            for t in range(first, last):
-                cols = slice(t * P, (t + 1) * P)
+        def weigh_on_scalar(t, dst):
+            for r in range(PACK):
+                nc.scalar.activation(dst.rearrange("p (k r) -> p r k", r=PACK)[:, r, :], turned[t][:, r, :], COPY, scale=weight[:, r : r + 1])
+
+        def multiply(first, count, u_bf, scales_tag):
+            u_words = held.tile([P, count * P], U32, name="u_words%d" % first, align_bytes=64)
+            u_scales = held.tile([P, count * P], U8, name="u_scales%d" % first, tag=scales_tag, align_bytes=64)
+            nc.vector.quantize_mx(u_words[:].bitcast(E5M2X4), u_scales[:], u_bf[:].rearrange("p t c -> p (t c)"))
+            for i in range(count):
+                cols = slice(i * P, (i + 1) * P)
                 nc.tensor.matmul_mx(
-                    moment[t],
+                    moment[first + i],
                     lhsT=u_words[:, cols].bitcast(E5M2X4),
                     lhsT_scale=u_scales[:, cols],
                     rhs=g_words[:].bitcast(E5M2X4),
@@ -126,37 +126,42 @@ def tile_list_moment_centred_stored_larger_pl_kernel(tc, xf, ra, gj_words, gj_sc
                     stop=True,
                 )
 
-        def keep_larger(sums_in_psum, first, last):
-            nc.vector.scalar_tensor_tensor(y[:, first:last, :], sums_in_psum, KEEP, old_kept[:, first:last, :], ALU.mult, ALU.max)
-            nc.sync.dma_start(out_dealt[:, first:last, :], y[:, first:last, :])
+        def keep_larger(dst, sums_in_psum, first, last):
+            nc.vector.scalar_tensor_tensor(dst, sums_in_psum, KEEP, old_kept[:, first:last, :], ALU.mult, ALU.max)
+            nc.sync.dma_start(out_dealt[:, first:last, :], dst)
 
         for t in range(PACK):
             gather(t)
-        for t in range(PACK):
-            nc.scalar.activation(old_kept[:, t, :], old_rows[:, t, :], COPY, scale=KEEP)
-        group_sums(0)
-        centre_and_turn(0)
-        group_sums(1)
-        turn_picked(2)
-        centre_and_turn(1)
+        for t in range(2):
+            turn_picked(t)
+            group_sums(t)
+            add_turned_means(t)
+        u_bf_0 = held.tile([P, 1, P * PACK], BF16, name="u_bf_0", align_bytes=64)
+        weigh(0, u_bf_0[:, 0, :])
         group_sums(2)
         turn_picked(3)
-        weigh(0)
-        add_turned_means(2)
+        centre_and_turn(2)
         group_sums(3)
-        weigh(1)
         add_turned_means(3)
-        multiply(0, 2)
-        weigh(2)
-        weigh(3)
-        multiply(2, 3)
-        multiply(3, 4)
-        keep_larger(moment_01[:], 0, 2)
-        nc.scalar.copy(y_bf[:, :, 0:2], y[:, 0:2, :].rearrange("p t n -> p n t"))
-        keep_larger(moment_2[:].unsqueeze(1), 2, 3)
-        keep_larger(moment_3[:].unsqueeze(1), 3, 4)
+        u_bf_1 = held.tile([P, 1, P * PACK], BF16, name="u_bf_1", tag="table3", align_bytes=64)
+        u_bf_23 = held.tile([P, 2, P * PACK], BF16, name="u_bf_23", tag="u_bf_23", align_bytes=64)
+        weigh_on_scalar(1, u_bf_1[:, 0, :])
+        multiply(0, 1, u_bf_0, "sums3")
+        multiply(1, 1, u_bf_1, "u_scales1")
+        old_kept = held.tile([P, PACK, N], F32, name="old_kept", tag="table3", align_bytes=64)
+        for t in range(PACK):
+            nc.scalar.activation(old_kept[:, t, :], old_rows[:, t, :], COPY, scale=KEEP)
+        weigh(2, u_bf_23[:, 0, :])
+        weigh(3, u_bf_23[:, 1, :])
+        multiply(2, 2, u_bf_23, "u_scales2")
+        y_01 = held.tile([P, 2, N], F32, name="y_01", tag="u_bf_23", align_bytes=64)
+        y_23 = held.tile([P, 2, N], F32, name="y_23")
+        keep_larger(y_01[:], moment_01[:], 0, 2)
+        nc.scalar.copy(y_bf[:, :, 0:2], y_01[:].rearrange("p t n -> p n t"))
+        keep_larger(y_23[:, 0:1, :], moment_2[:].unsqueeze(1), 2, 3)
+        keep_larger(y_23[:, 1:2, :], moment_3[:].unsqueeze(1), 3, 4)
 
-        nc.vector.tensor_copy(y_bf[:, :, 2:4], y[:, 2:4, :].rearrange("p t n -> p n t"))
+        nc.vector.tensor_copy(y_bf[:, :, 2:4], y_23[:].rearrange("p t n -> p n t"))
         y_words = held.tile([P, N], U32, name="y_words", align_bytes=64)
         y_scales = held.tile([P, N], U8, name="y_scales", align_bytes=64)
         nc.vector.quantize_mx(y_words[:].bitcast(E4M3X4), y_scales[:], y_bf[:].rearrange("p n t -> p (n t)"))

from contextlib import ExitStack

import concourse.mybir as mybir
from concourse.masks import make_identity

K, J, N, T = 512, 512, 256, 1024
FLOPS = 2 * K * J * N

F32 = mybir.dt.float32
BF16 = mybir.dt.bfloat16
I32 = mybir.dt.int32
U32 = mybir.dt.uint32
U16 = mybir.dt.uint16
U8 = mybir.dt.uint8
E5M2X4 = mybir.dt.float8_e5m2_x4
E4M3X4 = mybir.dt.float8_e4m3fn_x4
ALU = mybir.AluOpType
COPY = mybir.ActivationFunctionType.Copy

P = 128
PACK = 4
GROUP = 8
GROUPS = J // GROUP
KEEP = 0.04


def tile_list_moment_centred_stored_larger_pl_kernel(tc, xf, ra, gj_words, gj_scales, old, offs, out_0, out_1, out_2):
    nc = tc.nc
    with ExitStack() as ctx:
        held = ctx.enter_context(tc.tile_pool(name="held", bufs=1))
        psum = ctx.enter_context(tc.psum_pool(name="psum", bufs=1))

        offsets = held.tile([P, J // 16], U16, name="offsets")

        xf_dealt = xf.rearrange("(p t) c -> p t c", t=PACK)
        table = [held.tile([P, T], F32, name="table%d" % t, tag="table%d" % t, align_bytes=64) for t in range(PACK)]
        weight = held.tile([P, PACK], F32, name="weight")
        g_words = held.tile([P, N], U32, name="g_words", align_bytes=64)
        g_scales = held.tile([P, N], U8, name="g_scales", align_bytes=64)
        old_rows = held.tile([P, PACK, N], F32, name="old_rows")

        nc.vector.memset(g_scales[:].bitcast(U32), 0)
        nc.sync.dma_start(table[0][:], xf_dealt[:, 0, :])
        nc.sync.dma_start(offsets[:], offs)
        nc.sync.dma_start(weight[:], ra.rearrange("o (p r) -> (o p) r", r=PACK))
        for t in range(1, PACK):
            nc.sync.dma_start(table[t][:], xf_dealt[:, t, :])
        nc.sync.dma_start(g_words[:].bitcast(I32), gj_words[0].rearrange("p n r -> p (n r)").bitcast(I32))
        nc.sync.dma_start(old_rows[:], old.rearrange("(p t) n -> p t n", t=PACK))
        for q in range(4):
            nc.sync.dma_start(g_scales[32 * q : 32 * q + 4, :].bitcast(I32), gj_scales[0, 4 * q : 4 * q + 4, :].bitcast(I32))

        identity = held.tile([P, P], F32, name="identity")
        nc.any.memset(identity[:], 0.0)
        make_identity(nc, identity[:], nomemset=True)

        y_bf = held.tile([P, N, PACK], BF16, name="y_bf", align_bytes=64)
        out_dealt = out_0.rearrange("(p t) n -> p t n", t=PACK)

        picked = [held.tile([P, J], F32, name="picked%d" % t) for t in range(PACK)]
        sums = [held.tile([P, GROUPS], F32, name="sums%d" % t, tag="sums%d" % t, align_bytes=64) for t in range(PACK)]
        turned = [psum.tile([P, PACK, P], F32, name="turned%d" % t) for t in range(PACK)]
        moment_01 = psum.tile([P, 2, N], F32, name="moment_01")
        moment_2 = psum.tile([P, N], F32, name="moment_2")
        moment_3 = psum.tile([P, N], F32, name="moment_3")
        moment = [moment_01[:, 0, :], moment_01[:, 1, :], moment_2[:], moment_3[:]]

        def gather(t):
            if t == 0:
                half = J // 2
                nc.scalar.activation(picked[t][:, :half], table[t][:].indirect(offsets[:, : half // 16]), COPY)
                nc.vector.tensor_copy(picked[t][:, half:], table[t][:].indirect(offsets[:, half // 16 :]))
            else:
                nc.scalar.activation(picked[t][:], table[t][:].indirect(offsets[:]), COPY)

        def group_sums(t):
            nc.vector.tensor_reduce(sums[t][:], picked[t][:].rearrange("p (b i) -> p b i", i=GROUP), mybir.AxisListType.X, ALU.add)

        def centre_and_turn(t):
            centred = held.tile([P, 2, P, 2], F32, name="centred%d" % t)
            by_pair = picked[t][:].rearrange("p (q u e) -> p u q e", u=2, e=2)
            spread = sums[t][:].unsqueeze(2).to_broadcast([P, GROUPS, 4])
            for u in range(2):
                nc.vector.scalar_tensor_tensor(centred[:, u], spread, -1.0 / GROUP, by_pair[:, u], ALU.mult, ALU.add)
            for r in range(PACK):
                nc.tensor.transpose(turned[t][:, r, :], centred[:, r // 2, :, r % 2], identity[:])

        def turn_picked(t):
            by_slot = picked[t][:].rearrange("p (q r) -> p r q", r=PACK)
            for r in range(PACK):
                nc.tensor.matmul(turned[t][:, r, :], by_slot[:, r, :], identity[:], start=(r == 0), stop=False, is_transpose=True)

        def add_turned_means(t):
            less_mean = held.tile([P, GROUPS, 2], F32, name="less_mean%d" % t)
            nc.vector.tensor_scalar(less_mean[:], sums[t][:].unsqueeze(2).to_broadcast([P, GROUPS, 2]), -1.0 / GROUP, None, ALU.mult)
            for r in range(PACK):
                nc.tensor.matmul(
                    turned[t][:, r, :], less_mean[:].rearrange("p b h -> p (b h)"), identity[:], start=False, stop=(r == PACK - 1), is_transpose=True
                )

        def weigh(t, dst):
            nc.vector.tensor_tensor(
                dst.rearrange("p (k r) -> p k r", r=PACK),
                turned[t][:].rearrange("p r k -> p k r"),
                weight[:].unsqueeze(1).to_broadcast([P, P, PACK]),
                ALU.mult,
            )

        def weigh_on_scalar(t, dst):
            for r in range(PACK):
                nc.scalar.activation(dst.rearrange("p (k r) -> p r k", r=PACK)[:, r, :], turned[t][:, r, :], COPY, scale=weight[:, r : r + 1])

        def multiply(first, count, u_bf, scales_tag):
            u_words = held.tile([P, count * P], U32, name="u_words%d" % first, align_bytes=64)
            u_scales = held.tile([P, count * P], U8, name="u_scales%d" % first, tag=scales_tag, align_bytes=64)
            nc.vector.quantize_mx(u_words[:].bitcast(E5M2X4), u_scales[:], u_bf[:].rearrange("p t c -> p (t c)"))
            for i in range(count):
                cols = slice(i * P, (i + 1) * P)
                nc.tensor.matmul_mx(
                    moment[first + i],
                    lhsT=u_words[:, cols].bitcast(E5M2X4),
                    lhsT_scale=u_scales[:, cols],
                    rhs=g_words[:].bitcast(E5M2X4),
                    rhs_scale=g_scales[:],
                    start=True,
                    stop=True,
                )

        def keep_larger(dst, sums_in_psum, first, last):
            nc.vector.scalar_tensor_tensor(dst, sums_in_psum, KEEP, old_kept[:, first:last, :], ALU.mult, ALU.max)
            nc.sync.dma_start(out_dealt[:, first:last, :], dst)

        for t in range(PACK):
            gather(t)
        for t in range(2):
            turn_picked(t)
            group_sums(t)
            add_turned_means(t)
        u_bf_0 = held.tile([P, 1, P * PACK], BF16, name="u_bf_0", align_bytes=64)
        weigh(0, u_bf_0[:, 0, :])
        group_sums(2)
        turn_picked(3)
        centre_and_turn(2)
        group_sums(3)
        add_turned_means(3)
        u_bf_1 = held.tile([P, 1, P * PACK], BF16, name="u_bf_1", tag="table3", align_bytes=64)
        u_bf_23 = held.tile([P, 2, P * PACK], BF16, name="u_bf_23", tag="u_bf_23", align_bytes=64)
        weigh_on_scalar(1, u_bf_1[:, 0, :])
        multiply(0, 1, u_bf_0, "sums3")
        multiply(1, 1, u_bf_1, "u_scales1")
        old_kept = held.tile([P, PACK, N], F32, name="old_kept", tag="table3", align_bytes=64)
        for t in range(PACK):
            nc.scalar.activation(old_kept[:, t, :], old_rows[:, t, :], COPY, scale=KEEP)
        weigh(2, u_bf_23[:, 0, :])
        weigh(3, u_bf_23[:, 1, :])
        multiply(2, 2, u_bf_23, "u_scales2")
        y_01 = held.tile([P, 2, N], F32, name="y_01", tag="u_bf_23", align_bytes=64)
        y_23 = held.tile([P, 2, N], F32, name="y_23")
        keep_larger(y_01[:], moment_01[:], 0, 2)
        nc.scalar.copy(y_bf[:, :, 0:2], y_01[:].rearrange("p t n -> p n t"))
        keep_larger(y_23[:, 0:1, :], moment_2[:].unsqueeze(1), 2, 3)
        keep_larger(y_23[:, 1:2, :], moment_3[:].unsqueeze(1), 3, 4)

        nc.vector.tensor_copy(y_bf[:, :, 2:4], y_23[:].rearrange("p t n -> p n t"))
        y_words = held.tile([P, N], U32, name="y_words", align_bytes=64)
        y_scales = held.tile([P, N], U8, name="y_scales", align_bytes=64)
        nc.vector.quantize_mx(y_words[:].bitcast(E4M3X4), y_scales[:], y_bf[:].rearrange("p n t -> p (n t)"))
        nc.sync.dma_start(out_1[0].rearrange("p n r -> p (n r)").bitcast(I32), y_words[:].bitcast(I32))
        for q in range(4):
            queue = nc.scalar if q % 2 == 0 else nc.sync
            queue.dma_start(out_2[0, 4 * q : 4 * q + 4, :].bitcast(I32), y_scales[32 * q : 32 * q + 4, :].bitcast(I32))
